import numpy as np
import ml_dtypes


def mxq(x, axis, fmt="e4m3"):
    dtype, down = {"e4m3": (ml_dtypes.float8_e4m3fn, 7), "e5m2": (ml_dtypes.float8_e5m2, 14)}[fmt]
    v = np.moveaxis(np.asarray(x, np.float32).astype(ml_dtypes.bfloat16).astype(np.float64), axis, -1)
    blocks = v.reshape(v.shape[:-1] + (-1, 32))
    amax = np.abs(blocks).max(-1, keepdims=True)
    byte = np.maximum(np.where(amax > 0, np.frexp(amax)[1] - 1 + 127, 0) - down, 1)
    scale = np.exp2(byte - 127.0)
    codes = (blocks / scale).astype(np.float32).astype(dtype).astype(np.float64)
    return np.moveaxis((codes * scale).reshape(v.shape), -1, axis)


WIDE = False


def mx_kscale(k):
    if not WIDE:
        return np.ones(k)
    levels = np.array([10, -10, 5, -5, 0])
    if k % 512:
        return np.exp2(np.random.permutation(np.resize(levels, k // 32))).repeat(32)
    a = np.empty((k // 512, 16))
    for p in range(k // 512):
        a[p, :8] = np.random.permutation(np.resize(levels, 8))
        for g in range(8):
            far = levels[np.abs(levels - a[p, g]) >= 10]
            a[p, g + 8] = far[np.random.randint(len(far))]
    return np.exp2(a.ravel()).repeat(32)


def f64(x):
    return np.asarray(x).astype(np.float64)


def striped(idx):
    return np.tile(np.asarray(idx).reshape(-1, 16).T, (8, 1)).astype(np.uint16)


def unstriped(offs):
    return offs[:16].T.reshape(-1).astype(np.int64)


E2M1 = np.array([0.0, 0.5, 1.0, 1.5, 2.0, 3.0, 4.0, 6.0, -0.0, -0.5, -1.0, -1.5, -2.0, -3.0, -4.0, -6.0])


def pack_weight(w, fmt):
    k, n = w.shape
    w = f64(np.asarray(w, np.float32).astype(ml_dtypes.bfloat16)).reshape(k // 32, 32, n)
    amax = np.abs(w).max(1)
    if fmt == "e4m3":
        byte = np.frexp(amax)[1] - 1 + 127 - 7
    else:
        mant, ex = np.frexp(amax / 6.0)
        byte = np.where(mant > 0.5, ex, ex - 1) + 127
    byte = np.clip(np.where(amax > 0, byte, 1), 1, 254)
    scaled = (w * np.exp2(127.0 - byte)[:, None, :]).reshape(k, n).astype(np.float32)
    by_word = np.ascontiguousarray(scaled.reshape(k // 512, 128, 4, n).transpose(0, 1, 3, 2))
    if fmt == "e4m3":
        words = by_word.astype(ml_dtypes.float8_e4m3fn).view(np.uint8)
    else:
        c = by_word.astype(ml_dtypes.float4_e2m1fn).view(np.uint8) & 0xF
        words = (c[..., 0::2] | (c[..., 1::2] << 4)).reshape(k // 512, 128, 2 * n)
    return np.ascontiguousarray(words), np.ascontiguousarray(byte.astype(np.uint8).reshape(k // 512, 16, n))


def unpack_weight(words, scales, fmt):
    g, _, n = scales.shape
    words = np.ascontiguousarray(words).reshape(g, 128, n, -1)
    if fmt == "e4m3":
        vals = words.view(ml_dtypes.float8_e4m3fn).astype(np.float64)
    else:
        nib = np.empty((g, 128, n, 4), np.uint8)
        nib[..., 0::2] = words & 0xF
        nib[..., 1::2] = words >> 4
        vals = E2M1[nib]
    vals = vals * np.repeat(np.exp2(scales.astype(np.float64) - 127.0), 8, axis=1)[..., None]
    return vals.transpose(0, 1, 3, 2).reshape(g * 512, n)


D, E, U, T, I, G, Q = 512, 512, 512, 2048, 512, 64, 128


def setup_inputs():
    n = np.random.standard_normal
    idx = np.random.permutation(T)[:I]
    idx2 = np.random.permutation(U)[:G]
    fd = mx_kscale(D)
    fe = mx_kscale(E)
    keysp = pack_weight(n((D, T)) / fd[:, None], "e4m3")
    valsp = pack_weight(n((E, T)) / fe[:, None], "e4m3")
    return {
        "pquery": (n((D, Q)) * 0.8 / np.sqrt(D) * fd[:, None]).astype(np.float32),
        "pgsum": (n((D, U)) / fd[:, None]).astype(np.float32),
        "query": (n((D, Q)) * 0.7 / np.sqrt(D) * fd[:, None]).astype(np.float32),
        "keys_words": keysp[0],
        "keys_scales": keysp[1],
        "gout": (n((E, Q)) * 1 / np.sqrt(E) * fe[:, None]).astype(np.float32),
        "vals_words": valsp[0],
        "vals_scales": valsp[1],
        "dquery": (n((D, Q)) * 1.0 / np.sqrt(D) * fd[:, None]).astype(np.float32),
        "base": (0.5 * n((Q, I))).astype(np.float32),
        "offs": striped(idx),
        "offs2": striped(idx2),
    }


def reference(pquery, pgsum, query, keys_words, keys_scales, gout, vals_words, vals_scales, dquery, base, offs, offs2):
    idx = unstriped(offs)
    idx2 = unstriped(offs2)
    keysu = unpack_weight(keys_words, keys_scales, "e4m3")
    valsu = unpack_weight(vals_words, vals_scales, "e4m3")
    pqueryq = mxq(f64(pquery), 0, "e4m3")
    pgsumq = mxq(f64(pgsum), 0, "e4m3")
    b = pqueryq.T @ pgsumq
    m1 = np.max(b, axis=1, keepdims=True)
    pb = np.exp(b - m1)
    z = np.sum(pb, axis=1, keepdims=True)
    queryq = mxq(f64(query), 0, "e4m3")
    keysidxg = keysu[:, idx]
    a = queryq.T @ keysidxg
    dqueryq = mxq(f64(dquery), 0, "e4m3")
    ta = dqueryq.T @ keysidxg
    pa = np.exp(a)
    s = pa.reshape(Q, G, I // G).sum(axis=2)
    mo = np.exp(b[:, idx2] - m1)
    sh = mo / s
    sr = np.repeat(sh, I // G, axis=1)
    goutq = mxq(f64(gout), 0, "e4m3")
    valsidxg = valsu[:, idx]
    c1 = goutq.T @ valsidxg
    dsr = 1.0 / z * c1 * pa
    dsh = dsr.reshape(Q, G, I // G).sum(axis=2)
    ds = dsh * mo / np.square(s) * (-1.0)
    r1 = np.repeat(ds, I // G, axis=1)
    dpa = 1.0 / z * c1 * sr + r1
    xpa = ta * pa
    xs = xpa.reshape(Q, G, I // G).sum(axis=2)
    xsh = xs * mo / np.square(s) * (-1.0)
    xsr = np.repeat(xsh, I // G, axis=1)
    xdsr = xpa * 1.0 / z * c1
    xdsh = xdsr.reshape(Q, G, I // G).sum(axis=2)
    xds = (xdsh * mo - xs * s * 2.0 * dsh * mo / np.square(s)) / np.square(s) * (-1.0)
    xr1 = np.repeat(xds, I // G, axis=1)
    xdpa = xsr * 1.0 / z * c1 + xr1
    xda = xdpa * pa + xpa * dpa
    y = xda * 512.0 + f64(base)
    return y

@@ -1,0 +1,221 @@
+from contextlib import ExitStack
+
+import concourse.mybir as mybir
+from concourse.masks import make_identity
+
+F32 = mybir.dt.float32
+BF16 = mybir.dt.bfloat16
+I32 = mybir.dt.int32
+U32 = mybir.dt.uint32
+U16 = mybir.dt.uint16
+U8 = mybir.dt.uint8
+FP8X4 = mybir.dt.float8_e4m3fn_x4
+ALU = mybir.AluOpType
+ACT = mybir.ActivationFunctionType
+
+P = 128
+PACK = 4
+D, U, T, I, G, Q = 512, 512, 2048, 512, 64, 128
+J = I // G
+FLOPS = 2 * D * Q * (U + 3 * I)
+
+
+def tile_attend_hvopened_a_kernel(tc, pquery, pgsum, query, keys_words, keys_scales, gout, vals_words,
+                                   vals_scales, dquery, base, offs, offs2, out):
+    nc = tc.nc
+    with ExitStack() as ctx:
+        lists = ctx.enter_context(tc.tile_pool(name="lists", bufs=1))
+        sb = ctx.enter_context(tc.tile_pool(name="sb", bufs=1))
+        ps = ctx.enter_context(tc.psum_pool(name="ps", bufs=1))
+
+        def sbt(name, shape, dtype, tag=None):
+            return sb.tile(shape, dtype, name=name, tag=tag or name, align_bytes=64)
+
+        offs_t = lists.tile([P, I // 16], U16, name="offs_t")
+        offs2_t = lists.tile([P, G // 16], U16, name="offs2_t")
+
+        kw = sbt("kw", [P, T], U32)
+        vw = sbt("vw", [P, T], U32)
+        ks = sbt("ks", [P, T], U8)
+        vs = sbt("vs", [P, T], U8)
+        nc.gpsimd.memset(ks[:].bitcast(I32), 0)
+        nc.vector.memset(vs[:].bitcast(I32), 0)
+
+        def load_scales(eng, tile, scales, first):
+            for r in range(4):
+                eng.dma_start(out=tile[first + r:P:32, :].bitcast(I32), in_=scales[0][r:16:4, :].bitcast(I32))
+
+        def load_words(tile, words):
+            nc.sync.dma_start(out=tile[:].bitcast(I32), in_=words[0].rearrange("p n t -> p (n t)").bitcast(I32))
+
+        def load_rows(name, rows):
+            raw = sbt(name, [P, PACK, rows.shape[1]], F32)
+            nc.sync.dma_start(out=raw[:], in_=rows.rearrange("(p j) w -> p j w", j=PACK))
+            return raw
+
+        warm = sbt("warm", [P, 1], F32, "after_exp")
+        warm2 = sbt("warm2", [P, 1], F32)
+        nc.gpsimd.memset(warm[:], 0.0)
+
+        nc.sync.dma_start(offs_t[:], offs)
+        load_scales(nc.sync, ks, keys_scales, 0)
+        load_words(kw, keys_words)
+        nc.scalar.activation(warm2[:], warm[:], ACT.Exp)
+        q_raw = load_rows("q_raw", query)
+        dq_raw = load_rows("dq_raw", dquery)
+        load_scales(nc.sync, vs, vals_scales, 4)
+        load_words(vw, vals_words)
+        go_raw = load_rows("go_raw", gout)
+        pq_raw = load_rows("pq_raw", pquery)
+        pg_raw = [load_rows("pg_raw%d" % h, pgsum[:, h * 256:(h + 1) * 256]) for h in range(2)]
+        nc.sync.dma_start(offs2_t[:], offs2)
+        base_t = sbt("base_t", [P, I], F32)
+        nc.sync.dma_start(base_t[:], base)
+
+        ident = sbt("ident", [P, P], F32)
+        make_identity(nc, ident[:])
+
+        def weave(dst, raw):
+            nc.scalar.copy(out=dst.rearrange("p (c i t) -> p c t i", i=4, t=PACK),
+                           in_=raw[:].rearrange("p t (c i) -> p c t i", i=4))
+
+        def quantise(name, woven, width, tag=None):
+            codes = sbt(name + "_c", [P, width], U32, tag)
+            scales = sbt(name + "_s", [P, width], U8)
+            nc.vector.quantize_mx(out=codes[:].bitcast(FP8X4), scales=scales[:], in_=woven)
+            return codes, scales
+
+        def gather(name, window, dtype, tag=None):
+            got = sbt(name, [P, I], dtype, tag)
+            nc.vector.tensor_copy(got[:], window[:].indirect(offs_t[:]))
+            return got
+
+        def product(name, lhs, lhs_s, rhs, rhs_s):
+            acc = ps.tile([P, 512], F32, name=name)
+            nc.tensor.matmul_mx(out=acc[:], lhsT=lhs.bitcast(FP8X4), lhsT_scale=lhs_s, rhs=rhs.bitcast(FP8X4),
+                                rhs_scale=rhs_s, start=True, stop=True)
+            return acc
+
+        def dealt(bank):
+            return bank[:].rearrange("p (g j) -> p j g", j=J)
+
+        def by_page(ap):
+            return ap.rearrange("p (g j) -> p g j", j=J)
+
+        def spread(ap):
+            return ap.unsqueeze(2).to_broadcast([P, ap.shape[1], J])
+
+        def page_sums(name, pair):
+            turned = ps.tile([P, P], F32, name=name + "_t")
+            for j in range(J):
+                nc.tensor.matmul(turned[:], lhsT=pair[:, j, :], rhs=ident[:], is_transpose=True,
+                                 start=(j == 0), stop=(j == J - 1))
+            return turned
+
+        def turn_back(name, turned, copy, tag=None):
+            staged = sbt(name + "_s", [P, P], F32, tag)
+            copy(staged[:], turned[:])
+            back = ps.tile([P, P], F32, name=name + "_b")
+            nc.tensor.transpose(back[:], staged[:], ident[:])
+            return back
+
+        ksg = gather("ksg", ks, U8)
+        kwg = gather("kwg", kw, U32)
+        q_w = sbt("q_w", [P, Q * PACK], BF16)
+        dq_w = sbt("dq_w", [P, Q * PACK], BF16)
+        weave(q_w[:], q_raw)
+        weave(dq_w[:], dq_raw)
+        q_c, q_s = quantise("q", q_w[:], Q, "kw")
+        dq_c, dq_s = quantise("dq", dq_w[:], Q, "q_w")
+        a_ps = product("a_ps", q_c[:], q_s[:], kwg[:], ksg[:])
+        t_ps = product("t_ps", dq_c[:], dq_s[:], kwg[:], ksg[:])
+        vsg = gather("vsg", vs, U8, "dq_w")
+
+        x1 = sbt("x1", [P, J, 2 * G], F32)
+        nc.scalar.activation(x1[:, :, :G], dealt(a_ps), ACT.Exp, bias=warm[:])
+        nc.vector.tensor_tensor(x1[:, :, G:], dealt(t_ps), x1[:, :, :G], ALU.mult)
+        e_nat = sbt("e_nat", [P, I], F32)
+        nc.scalar.activation(e_nat[:], a_ps[:], ACT.Exp)
+        vwg = gather("vwg", vw, U32, "after_exp")
+        s1_t = page_sums("s1", x1)
+
+        go_w = sbt("go_w", [P, Q * PACK], BF16, "q_w")
+        weave(go_w[:], go_raw)
+        go_c, go_s = quantise("go", go_w[:], Q)
+        c_ps = product("c_ps", go_c[:], go_s[:], vwg[:], vsg[4:P, :])
+
+        x2 = sbt("x2", [P, J, 2 * G], F32)
+        for h in range(2):
+            js = slice(h * J // 2, (h + 1) * J // 2)
+            nc.vector.tensor_tensor(
+                x2[:, js, :].rearrange("p j (h g) -> p j h g", h=2),
+                dealt(c_ps)[:, js, :].unsqueeze(2).to_broadcast([P, J // 2, 2, G]),
+                x1[:, js, :].rearrange("p j (h g) -> p j h g", h=2), ALU.mult)
+            if h == 0:
+                s1 = turn_back("s1", s1_t, nc.vector.tensor_copy, "dq_w")
+        s2_t = page_sums("s2", x2)
+
+        rs = sbt("rs", [P, G], F32, "x1")
+        nc.vector.reciprocal(rs[:], s1[:, :G])
+        tbar = sbt("tbar", [P, G], F32)
+        nc.vector.tensor_tensor(tbar[:], s1[:, G:], rs[:], ALU.mult)
+        u = sbt("u", [P, I], F32)
+        nc.vector.tensor_tensor(by_page(u[:]), by_page(t_ps[:]), spread(tbar[:]), ALU.subtract)
+
+        pq_w = sbt("pq_w", [P, Q * PACK], BF16, "go_raw")
+        weave(pq_w[:], pq_raw)
+        pq_c, pq_s = quantise("pq", pq_w[:], Q)
+        pg_w = [sbt("pg_w0", [P, U * PACK // 2], BF16, "pq_raw"), sbt("pg_w1", [P, U * PACK // 2], BF16, "pg_raw0")]
+        pg_c = sbt("pg_c", [P, U], U32, "x2")
+        pg_s = sbt("pg_s", [P, U], U8)
+        for h in range(2):
+            weave(pg_w[h][:], pg_raw[h])
+            nc.vector.quantize_mx(out=pg_c[:, h * 256:(h + 1) * 256].bitcast(FP8X4),
+                                  scales=pg_s[:, h * 256:(h + 1) * 256], in_=pg_w[h][:])
+        s2 = turn_back("s2", s2_t, nc.scalar.copy)
+        b_ps = product("b_ps", pq_c[:], pq_s[:], pg_c[:], pg_s[:])
+
+        cw = sbt("cw", [P, 2 * G], F32)
+        nc.vector.tensor_tensor(cw[:].rearrange("p (h g) -> p h g", h=2), s2[:].rearrange("p (h g) -> p h g", h=2),
+                                rs[:].unsqueeze(1).to_broadcast([P, 2, G]), ALU.mult)
+        b_sb = sbt("b_sb", [P, U], F32)
+        m1 = sbt("m1", [P, 1], F32)
+        nc.vector.tensor_scalar(b_sb[:], b_ps[:], 1.0, None, ALU.mult, ALU.max, accum_out=m1[:])
+        v = sbt("v", [P, I], F32)
+        nc.vector.tensor_tensor(by_page(v[:]), by_page(c_ps[:]), spread(cw[:, :G]), ALU.subtract)
+        neg_m1 = sbt("neg_m1", [P, 1], F32)
+        nc.scalar.mul(neg_m1[:], m1[:], -1.0)
+        b_open = sbt("b_open", [P, G], F32)
+        nc.vector.tensor_copy(b_open[:], b_sb[:].indirect(offs2_t[:]))
+        pb = sbt("pb", [P, U], F32)
+        z = sbt("z", [P, 1], F32)
+        nc.scalar.activation(pb[:], b_sb[:], ACT.Exp, bias=neg_m1[:], accum_out=z[:])
+        mo = sbt("mo", [P, G], F32)
+        nc.scalar.activation(mo[:], b_open[:], ACT.Exp, bias=neg_m1[:])
+
+        tc_bar = sbt("tc_bar", [P, G], F32)
+        nc.vector.tensor_tensor(tc_bar[:], tbar[:], cw[:, :G], ALU.mult)
+        uv = sbt("uv", [P, I], F32)
+        nc.vector.tensor_tensor(uv[:], u[:], v[:], ALU.mult)
+        cov = sbt("cov", [P, G], F32)
+        nc.vector.tensor_tensor(cov[:], cw[:, G:], tc_bar[:], ALU.subtract)
+        halves = [slice(h * I // 2, (h + 1) * I // 2) for h in range(2)]
+        pages = [slice(h * G // 2, (h + 1) * G // 2) for h in range(2)]
+        y = sbt("y", [P, I], F32)
+        for cols, gs in zip(halves, pages):
+            nc.vector.tensor_tensor(by_page(y[:, cols]), by_page(uv[:, cols]), spread(cov[:, gs]), ALU.subtract)
+        ye = sbt("ye", [P, I], F32)
+        for cols in halves:
+            nc.vector.tensor_tensor(ye[:, cols], y[:, cols], e_nat[:, cols], ALU.mult)
+        rz = sbt("rz", [P, 1], F32)
+        nc.vector.reciprocal(rz[:], z[:])
+        alpha = sbt("alpha", [P, G], F32)
+        nc.vector.tensor_tensor(alpha[:], mo[:], rs[:], ALU.mult)
+        w = sbt("w", [P, I], F32)
+        for cols, gs in zip(halves, pages):
+            nc.vector.scalar_tensor_tensor(by_page(w[:, cols]), by_page(ye[:, cols]), rz[:], spread(alpha[:, gs]),
+                                           ALU.mult, ALU.mult)
+        for h, cols in enumerate(halves):
+            res = sbt("res%d" % h, [P, I // 2], F32)
+            nc.vector.scalar_tensor_tensor(res[:], w[:, cols], 512.0, base_t[:, cols], ALU.mult, ALU.add)
+            nc.sync.dma_start(out[:, cols], res[:])

@@ -53,19 +53,14 @@ def tile_attend_hvopened_a_kernel(tc, pquery, pgsum, query, keys_words, keys_sca
             nc.sync.dma_start(out=raw[:], in_=rows.rearrange("(p j) w -> p j w", j=PACK))
             return raw
 
-        warm = sbt("warm", [P, 1], F32, "after_exp")
-        warm2 = sbt("warm2", [P, 1], F32)
-        nc.gpsimd.memset(warm[:], 0.0)
-
         nc.sync.dma_start(offs_t[:], offs)
+        q_raw = load_rows("q_raw", query)
         load_scales(nc.sync, ks, keys_scales, 0)
         load_words(kw, keys_words)
-        nc.scalar.activation(warm2[:], warm[:], ACT.Exp)
-        q_raw = load_rows("q_raw", query)
         dq_raw = load_rows("dq_raw", dquery)
         load_scales(nc.sync, vs, vals_scales, 4)
-        load_words(vw, vals_words)
         go_raw = load_rows("go_raw", gout)
+        load_words(vw, vals_words)
         pq_raw = load_rows("pq_raw", pquery)
         pg_raw = [load_rows("pg_raw%d" % h, pgsum[:, h * 256:(h + 1) * 256]) for h in range(2)]
         nc.sync.dma_start(offs2_t[:], offs2)
@@ -76,8 +71,8 @@ def tile_attend_hvopened_a_kernel(tc, pquery, pgsum, query, keys_words, keys_sca
         make_identity(nc, ident[:])
 
         def weave(dst, raw):
-            nc.scalar.copy(out=dst.rearrange("p (c i t) -> p c t i", i=4, t=PACK),
-                           in_=raw[:].rearrange("p t (c i) -> p c t i", i=4))
+            nc.scalar.activation(dst.rearrange("p (c i t) -> p c t i", i=4, t=PACK),
+                                 raw[:].rearrange("p t (c i) -> p c t i", i=4), ACT.Copy)
 
         def quantise(name, woven, width, tag=None):
             codes = sbt(name + "_c", [P, width], U32, tag)
@@ -125,23 +120,23 @@ def tile_attend_hvopened_a_kernel(tc, pquery, pgsum, query, keys_words, keys_sca
         dq_w = sbt("dq_w", [P, Q * PACK], BF16)
         weave(q_w[:], q_raw)
         weave(dq_w[:], dq_raw)
-        q_c, q_s = quantise("q", q_w[:], Q, "kw")
-        dq_c, dq_s = quantise("dq", dq_w[:], Q, "q_w")
+        q_c, q_s = quantise("q", q_w[:], Q)
+        dq_c, dq_s = quantise("dq", dq_w[:], Q)
         a_ps = product("a_ps", q_c[:], q_s[:], kwg[:], ksg[:])
         t_ps = product("t_ps", dq_c[:], dq_s[:], kwg[:], ksg[:])
+        go_w = sbt("go_w", [P, Q * PACK], BF16)
+        weave(go_w[:], go_raw)
         vsg = gather("vsg", vs, U8, "dq_w")
+        go_c, go_s = quantise("go", go_w[:], Q)
 
-        x1 = sbt("x1", [P, J, 2 * G], F32)
-        nc.scalar.activation(x1[:, :, :G], dealt(a_ps), ACT.Exp, bias=warm[:])
+        x1 = sbt("x1", [P, J, 2 * G], F32, "go_raw")
+        nc.scalar.activation(x1[:, :, :G], dealt(a_ps), ACT.Exp)
         nc.vector.tensor_tensor(x1[:, :, G:], dealt(t_ps), x1[:, :, :G], ALU.mult)
-        e_nat = sbt("e_nat", [P, I], F32)
+        e_nat = sbt("e_nat", [P, I], F32, "go_w")
         nc.scalar.activation(e_nat[:], a_ps[:], ACT.Exp)
-        vwg = gather("vwg", vw, U32, "after_exp")
+        vwg = gather("vwg", vw, U32)
         s1_t = page_sums("s1", x1)
 
-        go_w = sbt("go_w", [P, Q * PACK], BF16, "q_w")
-        weave(go_w[:], go_raw)
-        go_c, go_s = quantise("go", go_w[:], Q)
         c_ps = product("c_ps", go_c[:], go_s[:], vwg[:], vsg[4:P, :])
 
         x2 = sbt("x2", [P, J, 2 * G], F32)
@@ -155,34 +150,36 @@ def tile_attend_hvopened_a_kernel(tc, pquery, pgsum, query, keys_words, keys_sca
                 s1 = turn_back("s1", s1_t, nc.vector.tensor_copy, "dq_w")
         s2_t = page_sums("s2", x2)
 
-        rs = sbt("rs", [P, G], F32, "x1")
+        rs = sbt("rs", [P, G], F32, "go_raw")
         nc.vector.reciprocal(rs[:], s1[:, :G])
         tbar = sbt("tbar", [P, G], F32)
         nc.vector.tensor_tensor(tbar[:], s1[:, G:], rs[:], ALU.mult)
         u = sbt("u", [P, I], F32)
         nc.vector.tensor_tensor(by_page(u[:]), by_page(t_ps[:]), spread(tbar[:]), ALU.subtract)
 
-        pq_w = sbt("pq_w", [P, Q * PACK], BF16, "go_raw")
+        pq_w = sbt("pq_w", [P, Q * PACK], BF16, "dq_c")
         weave(pq_w[:], pq_raw)
-        pq_c, pq_s = quantise("pq", pq_w[:], Q)
+        pq_c, pq_s = quantise("pq", pq_w[:], Q, "vw")
         pg_w = [sbt("pg_w0", [P, U * PACK // 2], BF16, "pq_raw"), sbt("pg_w1", [P, U * PACK // 2], BF16, "pg_raw0")]
-        pg_c = sbt("pg_c", [P, U], U32, "x2")
+        pg_c = sbt("pg_c", [P, U], U32)
         pg_s = sbt("pg_s", [P, U], U8)
         for h in range(2):
             weave(pg_w[h][:], pg_raw[h])
             nc.vector.quantize_mx(out=pg_c[:, h * 256:(h + 1) * 256].bitcast(FP8X4),
                                   scales=pg_s[:, h * 256:(h + 1) * 256], in_=pg_w[h][:])
-        s2 = turn_back("s2", s2_t, nc.scalar.copy)
+        s2 = turn_back("s2", s2_t, nc.scalar.copy, "pg_raw1")
         b_ps = product("b_ps", pq_c[:], pq_s[:], pg_c[:], pg_s[:])
 
         cw = sbt("cw", [P, 2 * G], F32)
-        nc.vector.tensor_tensor(cw[:].rearrange("p (h g) -> p h g", h=2), s2[:].rearrange("p (h g) -> p h g", h=2),
-                                rs[:].unsqueeze(1).to_broadcast([P, 2, G]), ALU.mult)
+        nc.vector.scalar_tensor_tensor(cw[:].rearrange("p (h g) -> p h g", h=2),
+                                       s2[:].rearrange("p (h g) -> p h g", h=2), 512.0,
+                                       rs[:].unsqueeze(1).to_broadcast([P, 2, G]), ALU.mult, ALU.mult)
         b_sb = sbt("b_sb", [P, U], F32)
         m1 = sbt("m1", [P, 1], F32)
         nc.vector.tensor_scalar(b_sb[:], b_ps[:], 1.0, None, ALU.mult, ALU.max, accum_out=m1[:])
         v = sbt("v", [P, I], F32)
-        nc.vector.tensor_tensor(by_page(v[:]), by_page(c_ps[:]), spread(cw[:, :G]), ALU.subtract)
+        nc.vector.scalar_tensor_tensor(by_page(v[:]), by_page(c_ps[:]), 512.0, spread(cw[:, :G]),
+                                       ALU.mult, ALU.subtract)
         neg_m1 = sbt("neg_m1", [P, 1], F32)
         nc.scalar.mul(neg_m1[:], m1[:], -1.0)
         b_open = sbt("b_open", [P, G], F32)
@@ -210,12 +207,11 @@ def tile_attend_hvopened_a_kernel(tc, pquery, pgsum, query, keys_words, keys_sca
         rz = sbt("rz", [P, 1], F32)
         nc.vector.reciprocal(rz[:], z[:])
         alpha = sbt("alpha", [P, G], F32)
-        nc.vector.tensor_tensor(alpha[:], mo[:], rs[:], ALU.mult)
+        nc.vector.scalar_tensor_tensor(alpha[:], mo[:], rz[:], rs[:], ALU.mult, ALU.mult)
         w = sbt("w", [P, I], F32)
         for cols, gs in zip(halves, pages):
-            nc.vector.scalar_tensor_tensor(by_page(w[:, cols]), by_page(ye[:, cols]), rz[:], spread(alpha[:, gs]),
-                                           ALU.mult, ALU.mult)
+            nc.vector.tensor_tensor(by_page(w[:, cols]), by_page(ye[:, cols]), spread(alpha[:, gs]), ALU.mult)
         for h, cols in enumerate(halves):
             res = sbt("res%d" % h, [P, I // 2], F32)
-            nc.vector.scalar_tensor_tensor(res[:], w[:, cols], 512.0, base_t[:, cols], ALU.mult, ALU.add)
+            nc.vector.tensor_tensor(res[:], w[:, cols], base_t[:, cols], ALU.add)
             nc.sync.dma_start(out[:, cols], res[:])

@@ -100,17 +100,18 @@ def tile_attend_hvopened_a_kernel(tc, pquery, pgsum, query, keys_words, keys_sca
         def spread(ap):
             return ap.unsqueeze(2).to_broadcast([P, ap.shape[1], J])
 
-        def page_sums(name, pair):
-            turned = ps.tile([P, P], F32, name=name + "_t")
-            for j in range(J):
-                nc.tensor.matmul(turned[:], lhsT=pair[:, j, :], rhs=ident[:], is_transpose=True,
-                                 start=(j == 0), stop=(j == J - 1))
+        def add_turned(name, blocks, bank):
+            turned = ps.tile([P, P], F32, name=name + "_t", tag=bank)
+            count = blocks.shape[1] // P
+            for j in range(count):
+                nc.tensor.matmul(turned[:], lhsT=blocks[:, j * P:(j + 1) * P], rhs=ident[:], is_transpose=True,
+                                 start=(j == 0), stop=(j == count - 1))
             return turned
 
-        def turn_back(name, turned, copy, tag=None):
+        def turn_back(name, turned, bank, tag=None):
             staged = sbt(name + "_s", [P, P], F32, tag)
-            copy(staged[:], turned[:])
-            back = ps.tile([P, P], F32, name=name + "_b")
+            nc.scalar.copy(staged[:], turned[:])
+            back = ps.tile([P, P], F32, name=name + "_b", tag=bank)
             nc.tensor.transpose(back[:], staged[:], ident[:])
             return back
 
@@ -129,37 +130,46 @@ def tile_attend_hvopened_a_kernel(tc, pquery, pgsum, query, keys_words, keys_sca
         vsg = gather("vsg", vs, U8, "dq_w")
         go_c, go_s = quantise("go", go_w[:], Q)
 
-        x1 = sbt("x1", [P, J, 2 * G], F32, "go_raw")
-        nc.scalar.activation(x1[:, :, :G], dealt(a_ps), ACT.Exp)
-        nc.vector.tensor_tensor(x1[:, :, G:], dealt(t_ps), x1[:, :, :G], ALU.mult)
+        x1 = sbt("x1", [P, 2 * I], F32, "go_raw")
+        e_dealt = x1[:, :I].rearrange("p (j g) -> p j g", j=J)
+        nc.scalar.activation(e_dealt, dealt(a_ps), ACT.Exp)
+        nc.vector.tensor_tensor(x1[:, I:].rearrange("p (j g) -> p j g", j=J), dealt(t_ps), e_dealt, ALU.mult)
         e_nat = sbt("e_nat", [P, I], F32, "go_w")
         nc.scalar.activation(e_nat[:], a_ps[:], ACT.Exp)
         vwg = gather("vwg", vw, U32)
-        s1_t = page_sums("s1", x1)
+        s_b = turn_back("s", add_turned("s", x1[:, :I], "turned0"), "back0")
+        ts_b = turn_back("ts", add_turned("ts", x1[:, I:], "turned1"), "back1")
 
         c_ps = product("c_ps", go_c[:], go_s[:], vwg[:], vsg[4:P, :])
 
-        x2 = sbt("x2", [P, J, 2 * G], F32)
+        def join(name, back, tag):
+            total = sbt(name, [P, G], F32, tag)
+            nc.vector.tensor_reduce(total[:], back[:].rearrange("p (r g) -> p g r", r=2), mybir.AxisListType.X,
+                                    ALU.add)
+            return total
+
+        s_sum = join("s_sum", s_b, "vw")
+        rs = sbt("rs", [P, G], F32)
+        nc.vector.reciprocal(rs[:], s_sum[:])
+
+        x2 = sbt("x2", [P, 2 * I], F32)
         for h in range(2):
             js = slice(h * J // 2, (h + 1) * J // 2)
             nc.vector.tensor_tensor(
-                x2[:, js, :].rearrange("p j (h g) -> p j h g", h=2),
+                x2[:].rearrange("p (j h g) -> p j h g", j=J, h=2)[:, js],
                 dealt(c_ps)[:, js, :].unsqueeze(2).to_broadcast([P, J // 2, 2, G]),
-                x1[:, js, :].rearrange("p j (h g) -> p j h g", h=2), ALU.mult)
-            if h == 0:
-                s1 = turn_back("s1", s1_t, nc.vector.tensor_copy, "dq_w")
-        s2_t = page_sums("s2", x2)
+                x1[:].rearrange("p (h j g) -> p j h g", j=J, h=2)[:, js], ALU.mult)
+        s2_t = add_turned("s2", x2[:], "turned0")
 
-        rs = sbt("rs", [P, G], F32, "go_raw")
-        nc.vector.reciprocal(rs[:], s1[:, :G])
+        ts_sum = join("ts_sum", ts_b, "go_raw")
         tbar = sbt("tbar", [P, G], F32)
-        nc.vector.tensor_tensor(tbar[:], s1[:, G:], rs[:], ALU.mult)
+        nc.vector.tensor_tensor(tbar[:], ts_sum[:], rs[:], ALU.mult)
         u = sbt("u", [P, I], F32)
         nc.vector.tensor_tensor(by_page(u[:]), by_page(t_ps[:]), spread(tbar[:]), ALU.subtract)
 
         pq_w = sbt("pq_w", [P, Q * PACK], BF16, "dq_c")
         weave(pq_w[:], pq_raw)
-        pq_c, pq_s = quantise("pq", pq_w[:], Q, "vw")
+        pq_c, pq_s = quantise("pq", pq_w[:], Q, "vwg")
         pg_w = [sbt("pg_w0", [P, U * PACK // 2], BF16, "pq_raw"), sbt("pg_w1", [P, U * PACK // 2], BF16, "pg_raw0")]
         pg_c = sbt("pg_c", [P, U], U32)
         pg_s = sbt("pg_s", [P, U], U8)
@@ -167,7 +177,7 @@ def tile_attend_hvopened_a_kernel(tc, pquery, pgsum, query, keys_words, keys_sca
             weave(pg_w[h][:], pg_raw[h])
             nc.vector.quantize_mx(out=pg_c[:, h * 256:(h + 1) * 256].bitcast(FP8X4),
                                   scales=pg_s[:, h * 256:(h + 1) * 256], in_=pg_w[h][:])
-        s2 = turn_back("s2", s2_t, nc.scalar.copy, "pg_raw1")
+        s2 = turn_back("s2", s2_t, "back0", "pg_raw1")
         b_ps = product("b_ps", pq_c[:], pq_s[:], pg_c[:], pg_s[:])
 
         cw = sbt("cw", [P, 2 * G], F32)
@@ -177,6 +187,8 @@ def tile_attend_hvopened_a_kernel(tc, pquery, pgsum, query, keys_words, keys_sca
         b_sb = sbt("b_sb", [P, U], F32)
         m1 = sbt("m1", [P, 1], F32)
         nc.vector.tensor_scalar(b_sb[:], b_ps[:], 1.0, None, ALU.mult, ALU.max, accum_out=m1[:])
+        tc_bar = sbt("tc_bar", [P, G], F32)
+        nc.vector.tensor_tensor(tc_bar[:], tbar[:], cw[:, :G], ALU.mult)
         v = sbt("v", [P, I], F32)
         nc.vector.scalar_tensor_tensor(by_page(v[:]), by_page(c_ps[:]), 512.0, spread(cw[:, :G]),
                                        ALU.mult, ALU.subtract)
@@ -189,25 +201,24 @@ def tile_attend_hvopened_a_kernel(tc, pquery, pgsum, query, keys_words, keys_sca
         nc.scalar.activation(pb[:], b_sb[:], ACT.Exp, bias=neg_m1[:], accum_out=z[:])
         mo = sbt("mo", [P, G], F32)
         nc.scalar.activation(mo[:], b_open[:], ACT.Exp, bias=neg_m1[:])
-
-        tc_bar = sbt("tc_bar", [P, G], F32)
-        nc.vector.tensor_tensor(tc_bar[:], tbar[:], cw[:, :G], ALU.mult)
-        uv = sbt("uv", [P, I], F32)
-        nc.vector.tensor_tensor(uv[:], u[:], v[:], ALU.mult)
         cov = sbt("cov", [P, G], F32)
         nc.vector.tensor_tensor(cov[:], cw[:, G:], tc_bar[:], ALU.subtract)
+
         halves = [slice(h * I // 2, (h + 1) * I // 2) for h in range(2)]
         pages = [slice(h * G // 2, (h + 1) * G // 2) for h in range(2)]
+        uv = sbt("uv", [P, I], F32)
+        for cols in halves:
+            nc.vector.tensor_tensor(uv[:, cols], u[:, cols], v[:, cols], ALU.mult)
+        rz = sbt("rz", [P, 1], F32)
+        nc.vector.reciprocal(rz[:], z[:])
         y = sbt("y", [P, I], F32)
         for cols, gs in zip(halves, pages):
             nc.vector.tensor_tensor(by_page(y[:, cols]), by_page(uv[:, cols]), spread(cov[:, gs]), ALU.subtract)
+        alpha = sbt("alpha", [P, G], F32)
+        nc.vector.scalar_tensor_tensor(alpha[:], mo[:], rz[:], rs[:], ALU.mult, ALU.mult)
         ye = sbt("ye", [P, I], F32)
         for cols in halves:
             nc.vector.tensor_tensor(ye[:, cols], y[:, cols], e_nat[:, cols], ALU.mult)
-        rz = sbt("rz", [P, 1], F32)
-        nc.vector.reciprocal(rz[:], z[:])
-        alpha = sbt("alpha", [P, G], F32)
-        nc.vector.scalar_tensor_tensor(alpha[:], mo[:], rz[:], rs[:], ALU.mult, ALU.mult)
         w = sbt("w", [P, I], F32)
         for cols, gs in zip(halves, pages):
             nc.vector.tensor_tensor(by_page(w[:, cols]), by_page(ye[:, cols]), spread(alpha[:, gs]), ALU.mult)

from contextlib import ExitStack

import concourse.mybir as mybir
from concourse.masks import make_identity

F32 = mybir.dt.float32
BF16 = mybir.dt.bfloat16
I32 = mybir.dt.int32
U32 = mybir.dt.uint32
U16 = mybir.dt.uint16
U8 = mybir.dt.uint8
FP8X4 = mybir.dt.float8_e4m3fn_x4
ALU = mybir.AluOpType
ACT = mybir.ActivationFunctionType

P = 128
PACK = 4
D, U, T, I, G, Q = 512, 512, 2048, 512, 64, 128
J = I // G
FLOPS = 2 * D * Q * (U + 3 * I)


def tile_attend_hvopened_a_kernel(tc, pquery, pgsum, query, keys_words, keys_scales, gout, vals_words,
                                   vals_scales, dquery, base, offs, offs2, out):
    nc = tc.nc
    with ExitStack() as ctx:
        lists = ctx.enter_context(tc.tile_pool(name="lists", bufs=1))
        sb = ctx.enter_context(tc.tile_pool(name="sb", bufs=1))
        ps = ctx.enter_context(tc.psum_pool(name="ps", bufs=1))

        def sbt(name, shape, dtype, tag=None):
            return sb.tile(shape, dtype, name=name, tag=tag or name, align_bytes=64)

        offs_t = lists.tile([P, I // 16], U16, name="offs_t")
        offs2_t = lists.tile([P, G // 16], U16, name="offs2_t")

        kw = sbt("kw", [P, T], U32)
        vw = sbt("vw", [P, T], U32)
        ks = sbt("ks", [P, T], U8)
        vs = sbt("vs", [P, T], U8)
        nc.gpsimd.memset(ks[:].bitcast(I32), 0)
        nc.vector.memset(vs[:].bitcast(I32), 0)

        def load_scales(eng, tile, scales, first):
            for r in range(4):
                eng.dma_start(out=tile[first + r:P:32, :].bitcast(I32), in_=scales[0][r:16:4, :].bitcast(I32))

        def load_words(tile, words):
            nc.sync.dma_start(out=tile[:].bitcast(I32), in_=words[0].rearrange("p n t -> p (n t)").bitcast(I32))

        def load_rows(name, rows):
            raw = sbt(name, [P, PACK, rows.shape[1]], F32)
            nc.sync.dma_start(out=raw[:], in_=rows.rearrange("(p j) w -> p j w", j=PACK))
            return raw

        nc.sync.dma_start(offs_t[:], offs)
        q_raw = load_rows("q_raw", query)
        load_scales(nc.sync, ks, keys_scales, 0)
        load_words(kw, keys_words)
        dq_raw = load_rows("dq_raw", dquery)
        load_scales(nc.sync, vs, vals_scales, 4)
        go_raw = load_rows("go_raw", gout)
        load_words(vw, vals_words)
        pq_raw = load_rows("pq_raw", pquery)
        pg_raw = [load_rows("pg_raw%d" % h, pgsum[:, h * 256:(h + 1) * 256]) for h in range(2)]
        nc.sync.dma_start(offs2_t[:], offs2)
        base_t = sbt("base_t", [P, I], F32)
        nc.sync.dma_start(base_t[:], base)

        ident = sbt("ident", [P, P], F32)
        make_identity(nc, ident[:])

        def weave(dst, raw):
            nc.scalar.activation(dst.rearrange("p (c i t) -> p c t i", i=4, t=PACK),
                                 raw[:].rearrange("p t (c i) -> p c t i", i=4), ACT.Copy)

        def quantise(name, woven, width, tag=None):
            codes = sbt(name + "_c", [P, width], U32, tag)
            scales = sbt(name + "_s", [P, width], U8)
            nc.vector.quantize_mx(out=codes[:].bitcast(FP8X4), scales=scales[:], in_=woven)
            return codes, scales

        def gather(name, window, dtype, tag=None):
            got = sbt(name, [P, I], dtype, tag)
            nc.vector.tensor_copy(got[:], window[:].indirect(offs_t[:]))
            return got

        def product(name, lhs, lhs_s, rhs, rhs_s):
            acc = ps.tile([P, 512], F32, name=name)
            nc.tensor.matmul_mx(out=acc[:], lhsT=lhs.bitcast(FP8X4), lhsT_scale=lhs_s, rhs=rhs.bitcast(FP8X4),
                                rhs_scale=rhs_s, start=True, stop=True)
            return acc

        def dealt(bank):
            return bank[:].rearrange("p (g j) -> p j g", j=J)

        def by_page(ap):
            return ap.rearrange("p (g j) -> p g j", j=J)

        def spread(ap):
            return ap.unsqueeze(2).to_broadcast([P, ap.shape[1], J])

        def add_turned(name, blocks, bank):
            turned = ps.tile([P, P], F32, name=name + "_t", tag=bank)
            count = blocks.shape[1] // P
            for j in range(count):
                nc.tensor.matmul(turned[:], lhsT=blocks[:, j * P:(j + 1) * P], rhs=ident[:], is_transpose=True,
                                 start=(j == 0), stop=(j == count - 1))
            return turned

        def turn_back(name, turned, bank, tag=None):
            staged = sbt(name + "_s", [P, P], F32, tag)
            nc.scalar.copy(staged[:], turned[:])
            back = ps.tile([P, P], F32, name=name + "_b", tag=bank)
            nc.tensor.transpose(back[:], staged[:], ident[:])
            return back

        ksg = gather("ksg", ks, U8)
        kwg = gather("kwg", kw, U32)
        q_w = sbt("q_w", [P, Q * PACK], BF16)
        dq_w = sbt("dq_w", [P, Q * PACK], BF16)
        weave(q_w[:], q_raw)
        weave(dq_w[:], dq_raw)
        q_c, q_s = quantise("q", q_w[:], Q)
        dq_c, dq_s = quantise("dq", dq_w[:], Q)
        a_ps = product("a_ps", q_c[:], q_s[:], kwg[:], ksg[:])
        t_ps = product("t_ps", dq_c[:], dq_s[:], kwg[:], ksg[:])
        go_w = sbt("go_w", [P, Q * PACK], BF16)
        weave(go_w[:], go_raw)
        vsg = gather("vsg", vs, U8, "dq_w")
        go_c, go_s = quantise("go", go_w[:], Q)

        x1 = sbt("x1", [P, 2 * I], F32, "go_raw")
        e_dealt = x1[:, :I].rearrange("p (j g) -> p j g", j=J)
        nc.scalar.activation(e_dealt, dealt(a_ps), ACT.Exp)
        nc.vector.tensor_tensor(x1[:, I:].rearrange("p (j g) -> p j g", j=J), dealt(t_ps), e_dealt, ALU.mult)
        e_nat = sbt("e_nat", [P, I], F32, "go_w")
        nc.scalar.activation(e_nat[:], a_ps[:], ACT.Exp)
        vwg = gather("vwg", vw, U32)
        s_b = turn_back("s", add_turned("s", x1[:, :I], "turned0"), "back0")
        ts_b = turn_back("ts", add_turned("ts", x1[:, I:], "turned1"), "back1")

        c_ps = product("c_ps", go_c[:], go_s[:], vwg[:], vsg[4:P, :])

        def join(name, back, tag):
            total = sbt(name, [P, G], F32, tag)
            nc.vector.tensor_reduce(total[:], back[:].rearrange("p (r g) -> p g r", r=2), mybir.AxisListType.X,
                                    ALU.add)
            return total

        s_sum = join("s_sum", s_b, "vw")
        rs = sbt("rs", [P, G], F32)
        nc.vector.reciprocal(rs[:], s_sum[:])

        x2 = sbt("x2", [P, 2 * I], F32)
        for h in range(2):
            js = slice(h * J // 2, (h + 1) * J // 2)
            nc.vector.tensor_tensor(
                x2[:].rearrange("p (j h g) -> p j h g", j=J, h=2)[:, js],
                dealt(c_ps)[:, js, :].unsqueeze(2).to_broadcast([P, J // 2, 2, G]),
                x1[:].rearrange("p (h j g) -> p j h g", j=J, h=2)[:, js], ALU.mult)
        s2_t = add_turned("s2", x2[:], "turned0")

        ts_sum = join("ts_sum", ts_b, "go_raw")
        tbar = sbt("tbar", [P, G], F32)
        nc.vector.tensor_tensor(tbar[:], ts_sum[:], rs[:], ALU.mult)
        u = sbt("u", [P, I], F32)
        nc.vector.tensor_tensor(by_page(u[:]), by_page(t_ps[:]), spread(tbar[:]), ALU.subtract)

        pq_w = sbt("pq_w", [P, Q * PACK], BF16, "dq_c")
        weave(pq_w[:], pq_raw)
        pq_c, pq_s = quantise("pq", pq_w[:], Q, "vwg")
        pg_w = [sbt("pg_w0", [P, U * PACK // 2], BF16, "pq_raw"), sbt("pg_w1", [P, U * PACK // 2], BF16, "pg_raw0")]
        pg_c = sbt("pg_c", [P, U], U32)
        pg_s = sbt("pg_s", [P, U], U8)
        for h in range(2):
            weave(pg_w[h][:], pg_raw[h])
            nc.vector.quantize_mx(out=pg_c[:, h * 256:(h + 1) * 256].bitcast(FP8X4),
                                  scales=pg_s[:, h * 256:(h + 1) * 256], in_=pg_w[h][:])
        s2 = turn_back("s2", s2_t, "back0", "pg_raw1")
        b_ps = product("b_ps", pq_c[:], pq_s[:], pg_c[:], pg_s[:])

        cw = sbt("cw", [P, 2 * G], F32)
        nc.vector.scalar_tensor_tensor(cw[:].rearrange("p (h g) -> p h g", h=2),
                                       s2[:].rearrange("p (h g) -> p h g", h=2), 512.0,
                                       rs[:].unsqueeze(1).to_broadcast([P, 2, G]), ALU.mult, ALU.mult)
        b_sb = sbt("b_sb", [P, U], F32)
        m1 = sbt("m1", [P, 1], F32)
        nc.vector.tensor_scalar(b_sb[:], b_ps[:], 1.0, None, ALU.mult, ALU.max, accum_out=m1[:])
        tc_bar = sbt("tc_bar", [P, G], F32)
        nc.vector.tensor_tensor(tc_bar[:], tbar[:], cw[:, :G], ALU.mult)
        v = sbt("v", [P, I], F32)
        nc.vector.scalar_tensor_tensor(by_page(v[:]), by_page(c_ps[:]), 512.0, spread(cw[:, :G]),
                                       ALU.mult, ALU.subtract)
        neg_m1 = sbt("neg_m1", [P, 1], F32)
        nc.scalar.mul(neg_m1[:], m1[:], -1.0)
        b_open = sbt("b_open", [P, G], F32)
        nc.vector.tensor_copy(b_open[:], b_sb[:].indirect(offs2_t[:]))
        pb = sbt("pb", [P, U], F32)
        z = sbt("z", [P, 1], F32)
        nc.scalar.activation(pb[:], b_sb[:], ACT.Exp, bias=neg_m1[:], accum_out=z[:])
        mo = sbt("mo", [P, G], F32)
        nc.scalar.activation(mo[:], b_open[:], ACT.Exp, bias=neg_m1[:])
        cov = sbt("cov", [P, G], F32)
        nc.vector.tensor_tensor(cov[:], cw[:, G:], tc_bar[:], ALU.subtract)

        halves = [slice(h * I // 2, (h + 1) * I // 2) for h in range(2)]
        pages = [slice(h * G // 2, (h + 1) * G // 2) for h in range(2)]
        uv = sbt("uv", [P, I], F32)
        for cols in halves:
            nc.vector.tensor_tensor(uv[:, cols], u[:, cols], v[:, cols], ALU.mult)
        rz = sbt("rz", [P, 1], F32)
        nc.vector.reciprocal(rz[:], z[:])
        y = sbt("y", [P, I], F32)
        for cols, gs in zip(halves, pages):
            nc.vector.tensor_tensor(by_page(y[:, cols]), by_page(uv[:, cols]), spread(cov[:, gs]), ALU.subtract)
        alpha = sbt("alpha", [P, G], F32)
        nc.vector.scalar_tensor_tensor(alpha[:], mo[:], rz[:], rs[:], ALU.mult, ALU.mult)
        ye = sbt("ye", [P, I], F32)
        for cols in halves:
            nc.vector.tensor_tensor(ye[:, cols], y[:, cols], e_nat[:, cols], ALU.mult)
        w = sbt("w", [P, I], F32)
        for cols, gs in zip(halves, pages):
            nc.vector.tensor_tensor(by_page(w[:, cols]), by_page(ye[:, cols]), spread(alpha[:, gs]), ALU.mult)
        for h, cols in enumerate(halves):
            res = sbt("res%d" % h, [P, I // 2], F32)
            nc.vector.tensor_tensor(res[:], w[:, cols], base_t[:, cols], ALU.add)
            nc.sync.dma_start(out[:, cols], res[:])
